import numpy as np, ml_dtypes
CORES = [24,40,56,80,88,96]
N = 6
import mx_ref
NC, KT, ROOT = 256, 2, 5
BF = ml_dtypes.bfloat16
def cut(t, i, w=512):
    return t[:, w * i:w * i + w]
def pk(c, s, i=0):
    return (np.ascontiguousarray(c[:, 512 * i:512 * i + 512]), mx_ref.live(s[:, 128 * i:128 * i + 128]))
def inputs(rng, e, E):
    def f(*shape):
        v = (rng.standard_normal(shape, dtype=np.float32) * np.exp2(rng.integers(-2, 3, shape[:-1] + (1,)))).astype(BF)
        return mx_ref.spread((v.astype(np.float32) * np.exp2(rng.integers(-E, E + 1, shape[:-2] + (1, 1))).astype(np.float32)).astype(BF), rng, e)
    def packed(k):
        c = np.zeros((N, 128, k * 512), np.uint8); s = np.zeros((N, 128, k * 128), np.uint8)
        for r in range(N):
            for i in range(k):
                a, b = mx_ref.quantize(f(128, 512)); c[r][:, 512 * i:512 * i + 512] = a; s[r][:, 128 * i:128 * i + 128] = mx_ref.plane(b, rng)
        return c, s
    d = {}
    d["wc"], d["ws"] = packed(KT)
    d["x"] = f(N, 128, KT * 4 * NC)
    return d
def setup_inputs(rng):
    return inputs(rng, 0, 0)
def setup_inputs_blocks(rng):
    return inputs(rng, 4, 0)
def setup_inputs_wide(rng):
    return inputs(rng, 0, 8)
def reference(wc, ws, x):
    y = np.zeros((N, 128, NC), np.float32)
    for r in range(N):
        for t in range(KT):
            p = mx_ref.matmul(pk(wc[ROOT], ws[ROOT], t), mx_ref.quantize(cut(x[r], t, 4 * NC)))
            y[r] = p if t == 0 else y[r] + p
    return {"y": y}

from concourse.bass import DstId, RemoteDMATransfer
from concourse.mybir import dt

KT = 2
WCOL = 128
XCOL = 256

SCRATCH = {
    "cD": ("dram", [128, KT * WCOL], "float8_e4m3fn_x4"),
    "sD": ("dram", [128, KT * WCOL], "uint8"),
    "wq": ("sbuf", [128, KT * WCOL], "float8_e4m3fn_x4"),
    "wp": ("sbuf", [128, KT * WCOL], "uint8"),
    "xb": ("sbuf", [128, KT * 4 * XCOL], "bfloat16"),
    "xq": ("sbuf", [128, KT * XCOL], "float8_e4m3fn_x4"),
    "xp": ("sbuf", [128, KT * XCOL], "uint8"),
    "yb": ("sbuf", [128, XCOL], "float32"),
    "ps": ("psum", [128, 512], "float32"),
}
SEMAPHORES = ["ls", "lc", "go", "hs", "hc", "sent", "warr", "xl0", "xl1", "q", "mm", "ev", "st"]


def _count(mask):
    return bin(mask).count("1")


def _lowest(mask, k):
    out, b = 0, 1
    while k > 0:
        if mask & b:
            out |= b
            k -= 1
        b <<= 1
    return out


def _plan(T, topo):
    root = T.cores[T.root]
    others = [c for c in T.cores if c != root]
    direct = [c for c in others if topo.may_write(root, c)]
    far = [c for c in others if not topo.may_write(root, c)]
    cand = [h for h in range(topo.CORES_PER_CHIP * topo.CHIPS)
            if topo.chip(h) == topo.chip(root) and h != root and T.rank_of(h) is None
            and all(topo.may_write(h, d) for d in far)]
    by_die = {}
    for h in cand:
        by_die.setdefault(topo.die(h), []).append(h)
    turn = []
    lists = [by_die[k] for k in sorted(by_die)]
    for i in range(max([len(v) for v in lists] + [0])):
        for v in lists:
            if i < len(v):
                turn.append(v[i])
    relay = {}
    for h, d in zip(turn, far):
        relay[h] = d
    return root, direct, relay


def _send(g, T, topo, src_core, dst_core, out_ap, in_ap, sem):
    rid, pid, _ = topo.addr(dst_core)
    m = topo.mask(src_core, dst_core)
    g.remote_dma(out_ap=out_ap, in_ap=in_ap, remote_sem=sem, local_sem=T.sem.sent, pid=pid, routing_id=rid,
                 dma_engine_mask=m)
    return _count(m)


def _compute(g, T, w_count):
    for t, sem in enumerate((T.sem.xl0, T.sem.xl1)):
        g.vector.wait_ge(sem, 16)
        g.vector.quantize_mx(T.xq[:, XCOL * t:XCOL * (t + 1)], T.xp[:, XCOL * t:XCOL * (t + 1)],
                             T.xb[:, 4 * XCOL * t:4 * XCOL * (t + 1)]).then_inc(T.sem.q, 1)
    g.tensor.wait_ge(T.sem.q, KT)
    g.tensor.wait_ge(T.sem.warr, w_count)
    for t in range(KT):
        mm = g.tensor.matmul_mx(T.ps[:, 0:XCOL],
                                T.wq[:, WCOL * t:WCOL * (t + 1)], T.wp[:, WCOL * t:WCOL * (t + 1)],
                                T.xq[:, XCOL * t:XCOL * (t + 1)], T.xp[:, XCOL * t:XCOL * (t + 1)],
                                t == 0, t == KT - 1)
    mm.then_inc(T.sem.mm, 1)
    g.vector.wait_ge(T.sem.mm, 1)
    g.vector.tensor_copy(T.yb[:], T.ps[:, 0:XCOL]).then_inc(T.sem.ev, 1)
    g.sync.wait_ge(T.sem.ev, 1)
    g.sync.dma_start(T.y[:], T.yb[:]).then_inc(T.sem.st, 16)
    g.sync.wait_ge(T.sem.st, 16)


def rank_program(g, core, T, topo):
    root, direct, relay = _plan(T, topo)
    half = 4 * XCOL
    cD, sD = T.cD[:].bitcast(dt.uint8), T.sD[:]
    wq, wp = T.wq[:].bitcast(dt.uint8), T.wp[:]

    if core in relay:
        dst = relay[core]
        on_chip = topo.mask(root, core)
        g.wait_ge(T.sem.hs, _count(_lowest(on_chip, 8)))
        left = _send(g, T, topo, core, dst, wp, sD, T.sem.warr)
        g.wait_ge(T.sem.hc, _count(on_chip))
        left += _send(g, T, topo, core, dst, wq, cD, T.sem.warr)
        g.wait_ge(T.sem.sent, left)
        return

    if T.rank_of(core) is None:
        return

    if core != root:
        g.sync.dma_start(T.xb[:, 0:half], T.x[:, 0:half]).then_inc(T.sem.xl0, 16)
        g.scalar.dma_start(T.xb[:, half:2 * half], T.x[:, half:2 * half]).then_inc(T.sem.xl1, 16)
        src = root if core in direct else [h for h in relay if relay[h] == core][0]
        _compute(g, T, 2 * _count(topo.mask(src, core)))
        return

    g.sync.dma_start(sD, T.ws[:]).then_inc(T.sem.ls, 16)
    g.sync.dma_start(cD, T.wc[:]).then_inc(T.sem.lc, 16)
    g.sync.sem_inc(T.sem.go, 1)
    g.sync.dma_start(T.xb[:, 0:half], T.x[:, 0:half]).then_inc(T.sem.xl0, 16)
    g.sync.dma_start(wp, T.ws[:]).then_inc(T.sem.warr, 16)
    g.scalar.wait_ge(T.sem.go, 1)
    g.scalar.dma_start(T.xb[:, half:2 * half], T.x[:, half:2 * half]).then_inc(T.sem.xl1, 16)
    g.scalar.dma_start(wq, T.wc[:]).then_inc(T.sem.warr, 16)

    relays = list(relay)
    left = 0
    ids = []
    on_chip = None
    for h in relays:
        rid, pid, _ = topo.addr(h)
        ids.append(DstId(rid=rid, pnc=pid))
        on_chip = topo.mask(root, h) if on_chip is None else on_chip & topo.mask(root, h)
    for load, buf, sem, m in ((T.sem.ls, sD, T.sem.hs, _lowest(on_chip, 8)), (T.sem.lc, cD, T.sem.hc, on_chip)):
        g.wait_ge(load, 16)
        g.remote_dma_fused([RemoteDMATransfer(dst_ids=ids, dma_engine_mask=m, remote_sem=sem,
                                              srcs=[buf], dsts=[buf for _ in relays])], local_sem=T.sem.sent)
        left += _count(m)
    for d in direct:
        left += _send(g, T, topo, root, d, wp, sD, T.sem.warr)
        left += _send(g, T, topo, root, d, wq, cD, T.sem.warr)
    _compute(g, T, 32)
    g.wait_ge(T.sem.sent, left)
